import numpy as np
import ml_dtypes


def mxq(x, axis, fmt="e4m3"):
    dtype, down = {"e4m3": (ml_dtypes.float8_e4m3fn, 7), "e5m2": (ml_dtypes.float8_e5m2, 14)}[fmt]
    v = np.moveaxis(np.asarray(x, np.float32).astype(ml_dtypes.bfloat16).astype(np.float64), axis, -1)
    blocks = v.reshape(v.shape[:-1] + (-1, 32))
    amax = np.abs(blocks).max(-1, keepdims=True)
    byte = np.maximum(np.where(amax > 0, np.frexp(amax)[1] - 1 + 127, 0) - down, 1)
    scale = np.exp2(byte - 127.0)
    codes = (blocks / scale).astype(np.float32).astype(dtype).astype(np.float64)
    return np.moveaxis((codes * scale).reshape(v.shape), -1, axis)


WIDE = False


def mx_kscale(k):
    if not WIDE:
        return np.ones(k)
    levels = np.array([10, -10, 5, -5, 0])
    if k % 512:
        return np.exp2(np.random.permutation(np.resize(levels, k // 32))).repeat(32)
    a = np.empty((k // 512, 16))
    for p in range(k // 512):
        a[p, :8] = np.random.permutation(np.resize(levels, 8))
        for g in range(8):
            far = levels[np.abs(levels - a[p, g]) >= 10]
            a[p, g + 8] = far[np.random.randint(len(far))]
    return np.exp2(a.ravel()).repeat(32)


def f64(x):
    return np.asarray(x).astype(np.float64)


def striped(idx):
    return np.tile(idx.reshape(-1, 16).T, (8, 1)).astype(np.uint16)


def unstriped(offs):
    return offs[:16].T.reshape(-1).astype(np.int64)


def striped8(idx):
    return np.concatenate([x.reshape(-1, 16).T for x in idx]).astype(np.uint16)


def runs(offs, k):
    lists = np.stack([offs[16 * r : 16 * r + 16].T.reshape(-1) for r in range(8)]).astype(np.int64)
    return lists[np.arange(k) % 512 // 64]


def pack_weight(w):
    k, n = w.shape
    w = f64(np.asarray(w, np.float32).astype(ml_dtypes.bfloat16)).reshape(k // 32, 32, n)
    amax = np.abs(w).max(1)
    byte = np.clip(np.where(amax > 0, np.frexp(amax)[1] - 1 + 127 - 7, 1), 1, 254)
    scaled = (w * np.exp2(127.0 - byte)[:, None, :]).reshape(k, n).astype(np.float32)
    words = np.ascontiguousarray(scaled.reshape(k // 512, 128, 4, n).transpose(0, 1, 3, 2)).astype(ml_dtypes.float8_e4m3fn).view(np.uint8)
    return words, np.ascontiguousarray(byte.astype(np.uint8).reshape(k // 512, 16, n))


def unpack_weight(words, scales):
    g, p, n, _ = words.shape
    vals = np.ascontiguousarray(words).view(ml_dtypes.float8_e4m3fn).astype(np.float64) * np.repeat(np.exp2(scales.astype(np.float64) - 127.0), 8, axis=1)[..., None]
    return vals.transpose(0, 1, 3, 2).reshape(g * 512, n)


def relu(v):
    return np.maximum(v, 0.0)


def sigmoid(v):
    return 1.0 / (1.0 + np.exp(-np.maximum(v, -700.0)))


K, T, S, G, H, C = 512, 1024, 512, 2048, 512, 512


def setup_inputs():
    n = np.random.standard_normal
    s = mx_kscale(K)[:, None]
    packed_xT = pack_weight(n((K, T)) * s)
    packed_dT = pack_weight(n((K, G)) / s)
    return {
        "x_words": packed_xT[0],
        "x_scales": packed_xT[1],
        "d_words": packed_dT[0],
        "d_scales": packed_dT[1],
        "gs": (np.random.uniform(0.5, 1.5, (K, 1)) / s).astype(np.float32),
        "offs": striped(np.random.permutation(T)[:S]),
        "k1": striped8(np.random.randint(0, G, (8, H))),
        "n1": striped8(np.stack([np.random.permutation(S) for _ in range(8)])),
        "n2": striped8(np.stack([np.random.permutation(S) for _ in range(8)])),
        "cand": striped(np.random.permutation(T)[:C]),
        "two": striped(np.random.permutation(T)[:S]),
        "k2": striped8(np.random.randint(0, G, (8, H))),
        "n3": striped8(np.stack([np.random.permutation(S) for _ in range(8)])),
        "n4": striped8(np.stack([np.random.permutation(S) for _ in range(8)])),
    }


def reference(x_words, x_scales, d_words, d_scales, gs, offs, k1, n1, n2, cand, two, k2, n3, n4):
    x_cand = unpack_weight(x_words, x_scales)[:, unstriped(cand)]
    d_k1 = unpack_weight(d_words, d_scales)[np.arange(K)[:, None], runs(k1, K)]
    xq = unpack_weight(x_words, x_scales)[:, unstriped(offs)]
    h = 0.0625 * (d_k1.T @ xq)
    pa = h - (h[np.arange(H)[:, None], runs(n1, H)])
    pb = h[np.arange(H)[:, None], runs(n2, H)] - h
    z = f64(gs) * (relu(np.minimum(pa, pb)) - (relu(-1.0 * np.maximum(pa, pb))))
    a = 0.0625 * ((x_cand.T @ mxq(z, 0, "e4m3")))
    d_k2 = unpack_weight(d_words, d_scales)[np.arange(K)[:, None], runs(k2, K)]
    x_two = unpack_weight(x_words, x_scales)[:, unstriped(two)]
    b = 0.0625 * (d_k2.T @ x_two)
    return a + (sigmoid(b[np.arange(H)[:, None], runs(n4, H)] - b)) * (a[np.arange(C)[:, None], runs(n3, C)] - a)

@@ -1,0 +1,200 @@
+from contextlib import ExitStack
+
+import concourse.mybir as mybir
+
+F32 = mybir.dt.float32
+BF16 = mybir.dt.bfloat16
+I32 = mybir.dt.int32
+U32 = mybir.dt.uint32
+U16 = mybir.dt.uint16
+U8 = mybir.dt.uint8
+FP8X4 = mybir.dt.float8_e4m3fn_x4
+ALU = mybir.AluOpType
+ACT = mybir.ActivationFunctionType
+
+P = 128
+N = 512
+TILES = 4
+HALF = 256
+TOKENS = 1024
+CODES = 2048
+FLOPS = 3 * 2 * 512 * 512 * 512
+
+
+def tile_picked_pqcjpullbminmod_none_p_kernel(tc, x_words, x_scales, d_words, d_scales, gs, offs, k1, n1, n2, cand, two, k2, n3, n4, out):
+    nc = tc.nc
+    with ExitStack() as ctx:
+        lists = ctx.enter_context(tc.tile_pool(name="lists", bufs=1))
+        keep = ctx.enter_context(tc.tile_pool(name="keep", bufs=1))
+        psum = ctx.enter_context(tc.psum_pool(name="psum", bufs=1))
+
+        def load_list(name, src):
+            t = lists.tile([P, N // 16], U16, name=name)
+            nc.sync.dma_start(t[:], src)
+            return t
+
+        def sb(name, width, dtype):
+            return keep.tile([P, width], dtype, name=name, align_bytes=64)
+
+        def half_list(t, hf):
+            return t[:, 16 * hf : 16 * (hf + 1)]
+
+        def cols(hf):
+            return slice(HALF * hf, HALF * (hf + 1))
+
+        k1_l = load_list("k1_l", k1)
+        d_sc = sb("d_sc", CODES, U8)
+        nc.sync.dma_start(
+            d_sc[:].bitcast(I32),
+            d_scales.rearrange("z q c -> q z c").bitcast(I32).to_broadcast([16, 8, CODES // 4]),
+        )
+        offs_l = load_list("offs_l", offs)
+        x_sc = sb("x_sc", TOKENS, U8)
+        nc.gpsimd.memset(x_sc[:].bitcast(I32), 0)
+        for q in range(4):
+            nc.scalar.dma_start(x_sc[32 * q : 32 * q + 4, :].bitcast(I32), x_scales[0, 4 * q : 4 * q + 4, :].bitcast(I32))
+        x_w = sb("x_w", TOKENS, U32)
+        nc.sync.dma_start(x_w[:].bitcast(I32), x_words[0].rearrange("p n t -> p (n t)").bitcast(I32))
+        d_w = sb("d_w", CODES, U32)
+        nc.sync.dma_start(d_w[:].bitcast(I32), d_words[0].rearrange("p n t -> p (n t)").bitcast(I32))
+        k2_l = load_list("k2_l", k2)
+        two_l = load_list("two_l", two)
+        cand_l = load_list("cand_l", cand)
+        gs_sb = sb("gs_sb", TILES, F32)
+        nc.sync.dma_start(gs_sb[:], gs.rearrange("(p t) o -> p (t o)", t=TILES))
+        n1_l = load_list("n1_l", n1)
+        n2_l = load_list("n2_l", n2)
+        n4_l = load_list("n4_l", n4)
+        n3_l = load_list("n3_l", n3)
+
+        gsc = sb("gsc", TILES, F32)
+        nc.gpsimd.tensor_scalar(gsc[:], gs_sb[:], 0.0625, 0.0, ALU.mult, ALU.add)
+
+        def gather(name, window, lst, dtype):
+            t = sb(name, N, dtype)
+            nc.vector.tensor_copy(t[:], window[:].indirect(lst[:]))
+            return t
+
+        def place_odd_rows(plane):
+            for j in range(1, 4):
+                nc.sync.dma_start(plane[j:P:32, :].bitcast(I32), plane[8 * j : P : 32, :].bitcast(I32))
+
+        def mx(bank, w, s, t, rw, rs):
+            m = slice(P * t, P * (t + 1))
+            nc.tensor.matmul_mx(out=bank, lhsT=w[:, m].bitcast(FP8X4), lhsT_scale=s[:, m], rhs=rw.bitcast(FP8X4), rhs_scale=rs, start=True, stop=True)
+
+        k1_bg = gather("k1_bg", d_sc, k1_l, U8)
+        k1_b = sb("k1_b", N, U8)
+        nc.vector.tensor_copy(
+            k1_b[:].rearrange("p (t c i) -> p c t i", t=4, i=16), k1_bg[:].rearrange("p (c i t) -> p c t i", t=4, i=16)
+        )
+        place_odd_rows(k1_b)
+        offs_w = gather("offs_w", x_w, offs_l, U32)
+        k1_wg = gather("k1_wg", d_w, k1_l, U32)
+        k1_w = sb("k1_w", N, U32)
+        nc.vector.tensor_copy(
+            k1_w[:].bitcast(I32).rearrange("p (t c i) -> p c t i", t=4, i=4),
+            k1_wg[:].bitcast(I32).rearrange("p (c i t) -> p c t i", t=4, i=4),
+        )
+        offs_b = gather("offs_b", x_sc, offs_l, U8)
+        h = []
+        for t in range(TILES):
+            bank = psum.tile([P, N], F32, name="bank_h", tag="bank%d" % t)
+            mx(bank[:], k1_w, k1_b, t, offs_w[:], offs_b[:])
+            h_t = sb("h%d" % t, N, F32)
+            nc.scalar.activation(h_t[:], bank[:], ACT.Copy, scale=gsc[:, t : t + 1])
+            h.append(h_t)
+
+        k2_bg = gather("k2_bg", d_sc, k2_l, U8)
+        k2_b = sb("k2_b", N, U8)
+        nc.vector.tensor_copy(
+            k2_b[:].bitcast(I32).rearrange("p (t c i) -> p c t i", t=4, i=2),
+            k2_bg[:].bitcast(I32).rearrange("p (c t i) -> p c t i", t=4, i=2),
+        )
+        place_odd_rows(k2_b)
+        two_b = gather("two_b", x_sc, two_l, U8)
+        two_w = gather("two_w", x_w, two_l, U32)
+        k2_wg = gather("k2_wg", d_w, k2_l, U32)
+        k2_w = sb("k2_w", N, U32)
+        nc.vector.tensor_copy(
+            k2_w[:].bitcast(I32).rearrange("p (t c i) -> p c t i", t=4, i=8),
+            k2_wg[:].bitcast(I32).rearrange("p (c t i) -> p c t i", t=4, i=8),
+        )
+        b_banks = []
+        for t in range(TILES):
+            bank = psum.tile([P, N], F32, name="bank_b", tag="bank%d" % (TILES + t))
+            mx(bank[:], k2_w, k2_b, t, two_w[:], two_b[:])
+            b_banks.append(bank)
+        cand_bg = gather("cand_bg", x_sc, cand_l, U8)
+        cand_b = sb("cand_b", N, U8)
+        nc.vector.tensor_copy(
+            cand_b[:].bitcast(I32).rearrange("p (t c i) -> p c t i", t=4, i=2),
+            cand_bg[:].bitcast(I32).rearrange("p (c t i) -> p c t i", t=4, i=2),
+        )
+        cand_w = sb("cand_w", N, U32)
+        nc.vector.tensor_copy(cand_w[:].rearrange("p (t c i) -> p c t i", t=4, i=8), x_w[:].indirect(cand_l[:]))
+
+        a_banks = [psum.tile([P, N], F32, name="bank_a", tag="bank%d" % t) for t in range(TILES)]
+        for hf in range(2):
+            pa = sb("pa%d" % hf, TILES * HALF, BF16)
+            pb = sb("pb%d" % hf, TILES * HALF, BF16)
+            for t in range(TILES):
+                g1 = sb("g1_%d_%d" % (hf, t), HALF, F32)
+                nc.scalar.activation(g1[:], h[t][:].indirect(half_list(n1_l, hf)), ACT.Copy)
+                g2 = sb("g2_%d_%d" % (hf, t), HALF, F32)
+                nc.scalar.activation(g2[:], h[t][:].indirect(half_list(n2_l, hf)), ACT.Copy)
+                nc.vector.tensor_tensor(pa[:, cols(t)], h[t][:, cols(hf)], g1[:], ALU.subtract)
+                nc.vector.tensor_tensor(pb[:, cols(t)], g2[:], h[t][:, cols(hf)], ALU.subtract)
+            lo = sb("lo%d" % hf, TILES * HALF, BF16)
+            hi = sb("hi%d" % hf, TILES * HALF, BF16)
+            nc.vector.tensor_scalar_min(lo[:], pa[:], 0.0)
+            nc.vector.tensor_scalar_max(hi[:], pa[:], 0.0)
+            up = sb("up%d" % hf, TILES * HALF, BF16)
+            nc.vector.tensor_tensor(up[:], pb[:], lo[:], ALU.max)
+            z = sb("z%d" % hf, TILES * HALF, BF16)
+            nc.vector.tensor_tensor(z[:], up[:], hi[:], ALU.min)
+            zi = sb("zi%d" % hf, TILES * HALF, BF16)
+            nc.vector.tensor_copy(
+                zi[:].rearrange("p (c i t) -> p c t i", t=4, i=4), z[:].rearrange("p (t c i) -> p c t i", t=4, i=4)
+            )
+            z_w = sb("z_w%d" % hf, HALF, U32)
+            z_b = sb("z_b%d" % hf, HALF, U8)
+            nc.vector.quantize_mx(out=z_w[:].bitcast(FP8X4), scales=z_b[:], in_=zi[:])
+            for t in range(TILES):
+                mx(a_banks[t][:, cols(hf)], cand_w, cand_b, t, z_w[:], z_b[:])
+
+        th = []
+        bs = []
+        for t in range(TILES):
+            b_t = sb("b%d" % t, N, F32)
+            nc.scalar.activation(b_t[:], b_banks[t][:], ACT.Copy, scale=0.0625)
+            bs.append(b_t)
+        for t in range(TILES):
+            g4 = sb("g4_%d" % t, N, F32)
+            for hf in range(2):
+                window = bs[t][:].indirect(half_list(n4_l, hf))
+                if t >= 2:
+                    nc.vector.tensor_copy(g4[:, cols(hf)], window)
+                else:
+                    nc.scalar.activation(g4[:, cols(hf)], window, ACT.Copy)
+            db = sb("db%d" % t, N, F32)
+            nc.vector.tensor_tensor(db[:], g4[:], bs[t][:], ALU.subtract)
+            th.append(db)
+
+        out_v = out.rearrange("(c t i) j -> t c i j", t=TILES, i=8)
+        for t in range(TILES):
+            a_t = sb("a%d" % t, N, F32)
+            nc.scalar.activation(a_t[:], a_banks[t][:], ACT.Copy, scale=0.03125)
+            th_t = sb("th%d" % t, N, F32)
+            nc.scalar.activation(th_t[:], th[t][:], ACT.Tanh, scale=0.5)
+            g3 = sb("g3_%d" % t, N, F32)
+            for hf in range(2):
+                nc.scalar.activation(g3[:, cols(hf)], a_t[:].indirect(half_list(n3_l, hf)), ACT.Copy)
+            da = sb("da%d" % t, N, F32)
+            mv = sb("mv%d" % t, N, F32)
+            o = sb("o%d" % t, N, F32)
+            for c in [cols(0), cols(1)] if t == TILES - 1 else [slice(0, N)]:
+                nc.vector.tensor_tensor(da[:, c], g3[:, c], a_t[:, c], ALU.subtract)
+                nc.vector.scalar_tensor_tensor(mv[:, c], th_t[:, c], 1.0, da[:, c], ALU.add, ALU.mult)
+                nc.vector.scalar_tensor_tensor(o[:, c], a_banks[t][:, c], 0.0625, mv[:, c], ALU.mult, ALU.add)
+                nc.sync.dma_start(out_v[t][:, :, c], o[:, c])

@@ -1,6 +1,7 @@
 from contextlib import ExitStack
 
 import concourse.mybir as mybir
+from concourse.masks import make_identity
 
 F32 = mybir.dt.float32
 BF16 = mybir.dt.bfloat16
@@ -33,8 +34,8 @@ def tile_picked_pqcjpullbminmod_none_p_kernel(tc, x_words, x_scales, d_words, d_
             nc.sync.dma_start(t[:], src)
             return t
 
-        def sb(name, width, dtype):
-            return keep.tile([P, width], dtype, name=name, align_bytes=64)
+        def sb(name, width, dtype, tag=""):
+            return keep.tile([P, width], dtype, name=name, tag=tag or name, align_bytes=64)
 
         def half_list(t, hf):
             return t[:, 16 * hf : 16 * (hf + 1)]
@@ -67,6 +68,8 @@ def tile_picked_pqcjpullbminmod_none_p_kernel(tc, x_words, x_scales, d_words, d_
         n4_l = load_list("n4_l", n4)
         n3_l = load_list("n3_l", n3)
 
+        ident = sb("ident", P, F32)
+        make_identity(nc, ident[:])
         gsc = sb("gsc", TILES, F32)
         nc.gpsimd.tensor_scalar(gsc[:], gs_sb[:], 0.0625, 0.0, ALU.mult, ALU.add)
 
@@ -135,6 +138,12 @@ def tile_picked_pqcjpullbminmod_none_p_kernel(tc, x_words, x_scales, d_words, d_
         nc.vector.tensor_copy(cand_w[:].rearrange("p (t c i) -> p c t i", t=4, i=8), x_w[:].indirect(cand_l[:]))
 
         a_banks = [psum.tile([P, N], F32, name="bank_a", tag="bank%d" % t) for t in range(TILES)]
+        z_mx = []
+
+        def a_product(hf):
+            for t in range(TILES):
+                mx(a_banks[t][:, cols(hf)], cand_w, cand_b, t, z_mx[hf][0][:], z_mx[hf][1][:])
+
         for hf in range(2):
             pa = sb("pa%d" % hf, TILES * HALF, BF16)
             pb = sb("pb%d" % hf, TILES * HALF, BF16)
@@ -147,54 +156,96 @@ def tile_picked_pqcjpullbminmod_none_p_kernel(tc, x_words, x_scales, d_words, d_
                 nc.vector.tensor_tensor(pb[:, cols(t)], g2[:], h[t][:, cols(hf)], ALU.subtract)
             lo = sb("lo%d" % hf, TILES * HALF, BF16)
             hi = sb("hi%d" % hf, TILES * HALF, BF16)
-            nc.vector.tensor_scalar_min(lo[:], pa[:], 0.0)
-            nc.vector.tensor_scalar_max(hi[:], pa[:], 0.0)
             up = sb("up%d" % hf, TILES * HALF, BF16)
-            nc.vector.tensor_tensor(up[:], pb[:], lo[:], ALU.max)
             z = sb("z%d" % hf, TILES * HALF, BF16)
-            nc.vector.tensor_tensor(z[:], up[:], hi[:], ALU.min)
             zi = sb("zi%d" % hf, TILES * HALF, BF16)
-            nc.vector.tensor_copy(
-                zi[:].rearrange("p (c i t) -> p c t i", t=4, i=4), z[:].rearrange("p (t c i) -> p c t i", t=4, i=4)
-            )
             z_w = sb("z_w%d" % hf, HALF, U32)
             z_b = sb("z_b%d" % hf, HALF, U8)
-            nc.vector.quantize_mx(out=z_w[:].bitcast(FP8X4), scales=z_b[:], in_=zi[:])
-            for t in range(TILES):
-                mx(a_banks[t][:, cols(hf)], cand_w, cand_b, t, z_w[:], z_b[:])
+            pieces = hf + 1
+            width = HALF // pieces
 
-        th = []
-        bs = []
+            def part(tile, k):
+                return tile[:].rearrange("p (t j) -> p t j", t=TILES)[:, :, width * k : width * (k + 1)]
+
+            for k in range(pieces):
+                nc.vector.tensor_scalar_min(part(lo, k), part(pa, k), 0.0)
+                nc.vector.tensor_scalar_max(part(hi, k), part(pa, k), 0.0)
+            for k in range(pieces):
+                nc.vector.tensor_tensor(part(up, k), part(pb, k), part(lo, k), ALU.max)
+            for k in range(pieces):
+                nc.vector.tensor_tensor(part(z, k), part(up, k), part(hi, k), ALU.min)
+            for k in range(pieces):
+                nc.vector.tensor_copy(
+                    zi[:, 4 * width * k : 4 * width * (k + 1)].rearrange("p (c i t) -> p c t i", t=4, i=4),
+                    part(z, k).rearrange("p t (c i) -> p c t i", i=4),
+                )
+            for k in range(pieces):
+                c = slice(width * k, width * (k + 1))
+                nc.vector.quantize_mx(out=z_w[:, c].bitcast(FP8X4), scales=z_b[:, c], in_=zi[:, 4 * width * k : 4 * width * (k + 1)])
+            z_mx.append((z_w, z_b))
+            if hf == 0:
+                a_product(0)
+
+        def block(k):
+            return slice(P * k, P * (k + 1))
+
+        bn = []
         for t in range(TILES):
-            b_t = sb("b%d" % t, N, F32)
-            nc.scalar.activation(b_t[:], b_banks[t][:], ACT.Copy, scale=0.0625)
-            bs.append(b_t)
-        for t in range(TILES):
-            g4 = sb("g4_%d" % t, N, F32)
+            bn_t = sb("bn%d" % t, N, F32)
+            nc.scalar.activation(bn_t[:], b_banks[t][:], ACT.Copy, scale=-0.0625)
+            bn.append(bn_t)
+        g4_slots = ["", "z1", "zi1", "z_w1"]
+        db_banks = []
+        a_half = [sb("a%d" % t, N, F32) for t in range(TILES)]
+
+        def gate(t):
+            g4 = sb("g4_%d" % t, N, F32, tag=g4_slots[t])
             for hf in range(2):
-                window = bs[t][:].indirect(half_list(n4_l, hf))
-                if t >= 2:
-                    nc.vector.tensor_copy(g4[:, cols(hf)], window)
+                window = bn[t][:].indirect(half_list(n4_l, hf))
+                if t in (0, 3):
+                    nc.scalar.activation(g4[:, cols(hf)], window, ACT.Copy, scale=-1.0)
                 else:
-                    nc.scalar.activation(g4[:, cols(hf)], window, ACT.Copy)
-            db = sb("db%d" % t, N, F32)
-            nc.vector.tensor_tensor(db[:], g4[:], bs[t][:], ALU.subtract)
-            th.append(db)
+                    nc.vector.tensor_scalar(g4[:, cols(hf)], window, -1.0, 0.0, ALU.mult, ALU.add)
+            bank = psum.tile([P, N], F32, name="bank_db", tag="bank%d" % (TILES + t))
+            for k in range(TILES):
+                nc.tensor.matmul(bank[:, block(k)], lhsT=bn[t][:, block(k)], rhs=ident[:], is_transpose=True, start=True, stop=False)
+                nc.tensor.matmul(bank[:, block(k)], lhsT=g4[:, block(k)], rhs=ident[:], is_transpose=True, start=False, stop=True)
+            db_banks.append(bank)
 
         out_v = out.rearrange("(c t i) j -> t c i j", t=TILES, i=8)
-        for t in range(TILES):
-            a_t = sb("a%d" % t, N, F32)
-            nc.scalar.activation(a_t[:], a_banks[t][:], ACT.Copy, scale=0.03125)
-            th_t = sb("th%d" % t, N, F32)
-            nc.scalar.activation(th_t[:], th[t][:], ACT.Tanh, scale=0.5)
+
+        def finish(t):
+            a_t = a_half[t]
+            nc.scalar.activation(a_t[:, cols(1)], a_banks[t][:, cols(1)], ACT.Copy, scale=0.03125)
+            th_t = sb("th%d" % t, N, F32, tag="z_b1" if t == 0 else "")
+            nc.scalar.activation(th_t[:], db_banks[t][:], ACT.Tanh, scale=0.5)
+            th_bank = psum.tile([P, N], F32, name="bank_th", tag="bank%d" % (TILES + t))
+            for k in range(TILES):
+                nc.tensor.transpose(th_bank[:, block(k)], th_t[:, block(k)], ident[:])
             g3 = sb("g3_%d" % t, N, F32)
             for hf in range(2):
                 nc.scalar.activation(g3[:, cols(hf)], a_t[:].indirect(half_list(n3_l, hf)), ACT.Copy)
             da = sb("da%d" % t, N, F32)
             mv = sb("mv%d" % t, N, F32)
             o = sb("o%d" % t, N, F32)
-            for c in [cols(0), cols(1)] if t == TILES - 1 else [slice(0, N)]:
-                nc.vector.tensor_tensor(da[:, c], g3[:, c], a_t[:, c], ALU.subtract)
-                nc.vector.scalar_tensor_tensor(mv[:, c], th_t[:, c], 1.0, da[:, c], ALU.add, ALU.mult)
-                nc.vector.scalar_tensor_tensor(o[:, c], a_banks[t][:, c], 0.0625, mv[:, c], ALU.mult, ALU.add)
-                nc.sync.dma_start(out_v[t][:, :, c], o[:, c])
+            for hf in range(2):
+                nc.vector.tensor_tensor(da[:, cols(hf)], g3[:, cols(hf)], a_t[:, cols(hf)], ALU.subtract)
+            for hf in range(2):
+                nc.vector.scalar_tensor_tensor(mv[:, cols(hf)], th_bank[:, cols(hf)], 1.0, da[:, cols(hf)], ALU.add, ALU.mult)
+            for hf in range(2):
+                nc.vector.scalar_tensor_tensor(o[:, cols(hf)], a_banks[t][:, cols(hf)], 0.0625, mv[:, cols(hf)], ALU.mult, ALU.add)
+                if t == TILES - 1:
+                    nc.sync.dma_start(out_v[t][:, :, cols(hf)], o[:, cols(hf)])
+            if t < TILES - 1:
+                nc.sync.dma_start(out_v[t], o[:])
+
+        gate(0)
+        for t in range(TILES):
+            nc.scalar.activation(a_half[t][:, cols(0)], a_banks[t][:, cols(0)], ACT.Copy, scale=0.03125)
+        a_product(1)
+        gate(1)
+        gate(2)
+        finish(0)
+        gate(3)
+        for t in range(1, TILES):
+            finish(t)

@@ -1,7 +1,6 @@
 from contextlib import ExitStack
 
 import concourse.mybir as mybir
-from concourse.masks import make_identity
 
 F32 = mybir.dt.float32
 BF16 = mybir.dt.bfloat16
@@ -50,26 +49,26 @@ def tile_picked_pqcjpullbminmod_none_p_kernel(tc, x_words, x_scales, d_words, d_
             d_scales.rearrange("z q c -> q z c").bitcast(I32).to_broadcast([16, 8, CODES // 4]),
         )
         offs_l = load_list("offs_l", offs)
-        x_sc = sb("x_sc", TOKENS, U8)
-        nc.gpsimd.memset(x_sc[:].bitcast(I32), 0)
-        for q in range(4):
-            nc.scalar.dma_start(x_sc[32 * q : 32 * q + 4, :].bitcast(I32), x_scales[0, 4 * q : 4 * q + 4, :].bitcast(I32))
         x_w = sb("x_w", TOKENS, U32)
         nc.sync.dma_start(x_w[:].bitcast(I32), x_words[0].rearrange("p n t -> p (n t)").bitcast(I32))
         d_w = sb("d_w", CODES, U32)
         nc.sync.dma_start(d_w[:].bitcast(I32), d_words[0].rearrange("p n t -> p (n t)").bitcast(I32))
+        x_sc = sb("x_sc", TOKENS, U8)
+        for q in range(4):
+            nc.sync.dma_start(
+                x_sc[32 * q : 32 * (q + 1), :].bitcast(I32),
+                x_scales[:, 4 * q : 4 * q + 4, :].bitcast(I32).to_broadcast([8, 4, TOKENS // 4]),
+            )
         k2_l = load_list("k2_l", k2)
         two_l = load_list("two_l", two)
         cand_l = load_list("cand_l", cand)
         gs_sb = sb("gs_sb", TILES, F32)
-        nc.sync.dma_start(gs_sb[:], gs.rearrange("(p t) o -> p (t o)", t=TILES))
+        nc.gpsimd.dma_start(gs_sb[:], gs.rearrange("(p t) o -> p (t o)", t=TILES))
         n1_l = load_list("n1_l", n1)
         n2_l = load_list("n2_l", n2)
         n4_l = load_list("n4_l", n4)
         n3_l = load_list("n3_l", n3)
 
-        ident = sb("ident", P, F32)
-        make_identity(nc, ident[:])
         gsc = sb("gsc", TILES, F32)
         nc.gpsimd.tensor_scalar(gsc[:], gs_sb[:], 0.0625, 0.0, ALU.mult, ALU.add)
 
@@ -78,9 +77,9 @@ def tile_picked_pqcjpullbminmod_none_p_kernel(tc, x_words, x_scales, d_words, d_
             nc.vector.tensor_copy(t[:], window[:].indirect(lst[:]))
             return t
 
-        def place_odd_rows(plane):
+        def place_odd_rows(plane, queue):
             for j in range(1, 4):
-                nc.sync.dma_start(plane[j:P:32, :].bitcast(I32), plane[8 * j : P : 32, :].bitcast(I32))
+                queue.dma_start(plane[j:P:32, :].bitcast(I32), plane[8 * j : P : 32, :].bitcast(I32))
 
         def mx(bank, w, s, t, rw, rs):
             m = slice(P * t, P * (t + 1))
@@ -91,7 +90,7 @@ def tile_picked_pqcjpullbminmod_none_p_kernel(tc, x_words, x_scales, d_words, d_
         nc.vector.tensor_copy(
             k1_b[:].rearrange("p (t c i) -> p c t i", t=4, i=16), k1_bg[:].rearrange("p (c i t) -> p c t i", t=4, i=16)
         )
-        place_odd_rows(k1_b)
+        place_odd_rows(k1_b, nc.scalar)
         offs_w = gather("offs_w", x_w, offs_l, U32)
         k1_wg = gather("k1_wg", d_w, k1_l, U32)
         k1_w = sb("k1_w", N, U32)
@@ -108,32 +107,32 @@ def tile_picked_pqcjpullbminmod_none_p_kernel(tc, x_words, x_scales, d_words, d_
             nc.scalar.activation(h_t[:], bank[:], ACT.Copy, scale=gsc[:, t : t + 1])
             h.append(h_t)
 
-        k2_bg = gather("k2_bg", d_sc, k2_l, U8)
-        k2_b = sb("k2_b", N, U8)
-        nc.vector.tensor_copy(
-            k2_b[:].bitcast(I32).rearrange("p (t c i) -> p c t i", t=4, i=2),
-            k2_bg[:].bitcast(I32).rearrange("p (c t i) -> p c t i", t=4, i=2),
-        )
-        place_odd_rows(k2_b)
-        two_b = gather("two_b", x_sc, two_l, U8)
-        two_w = gather("two_w", x_w, two_l, U32)
         k2_wg = gather("k2_wg", d_w, k2_l, U32)
+        k2_bg = gather("k2_bg", d_sc, k2_l, U8)
+        cand_bg = gather("cand_bg", x_sc, cand_l, U8)
         k2_w = sb("k2_w", N, U32)
         nc.vector.tensor_copy(
             k2_w[:].bitcast(I32).rearrange("p (t c i) -> p c t i", t=4, i=8),
             k2_wg[:].bitcast(I32).rearrange("p (c t i) -> p c t i", t=4, i=8),
         )
-        b_banks = []
-        for t in range(TILES):
-            bank = psum.tile([P, N], F32, name="bank_b", tag="bank%d" % (TILES + t))
-            mx(bank[:], k2_w, k2_b, t, two_w[:], two_b[:])
-            b_banks.append(bank)
-        cand_bg = gather("cand_bg", x_sc, cand_l, U8)
+        k2_b = sb("k2_b", N, U8)
+        nc.vector.tensor_copy(
+            k2_b[:].bitcast(I32).rearrange("p (t c i) -> p c t i", t=4, i=2),
+            k2_bg[:].bitcast(I32).rearrange("p (c t i) -> p c t i", t=4, i=2),
+        )
+        place_odd_rows(k2_b, nc.sync)
         cand_b = sb("cand_b", N, U8)
         nc.vector.tensor_copy(
             cand_b[:].bitcast(I32).rearrange("p (t c i) -> p c t i", t=4, i=2),
             cand_bg[:].bitcast(I32).rearrange("p (c t i) -> p c t i", t=4, i=2),
         )
+        two_b = gather("two_b", x_sc, two_l, U8)
+        two_w = gather("two_w", x_w, two_l, U32)
+        b_banks = []
+        for t in range(TILES):
+            bank = psum.tile([P, N], F32, name="bank_b", tag="bank%d" % (TILES + t))
+            mx(bank[:], k2_w, k2_b, t, two_w[:], two_b[:])
+            b_banks.append(bank)
         cand_w = sb("cand_w", N, U32)
         nc.vector.tensor_copy(cand_w[:].rearrange("p (t c i) -> p c t i", t=4, i=8), x_w[:].indirect(cand_l[:]))
 
@@ -149,20 +148,24 @@ def tile_picked_pqcjpullbminmod_none_p_kernel(tc, x_words, x_scales, d_words, d_
             pb = sb("pb%d" % hf, TILES * HALF, BF16)
             for t in range(TILES):
                 g1 = sb("g1_%d_%d" % (hf, t), HALF, F32)
-                nc.scalar.activation(g1[:], h[t][:].indirect(half_list(n1_l, hf)), ACT.Copy)
                 g2 = sb("g2_%d_%d" % (hf, t), HALF, F32)
-                nc.scalar.activation(g2[:], h[t][:].indirect(half_list(n2_l, hf)), ACT.Copy)
-                nc.vector.tensor_tensor(pa[:, cols(t)], h[t][:, cols(hf)], g1[:], ALU.subtract)
-                nc.vector.tensor_tensor(pb[:, cols(t)], g2[:], h[t][:, cols(hf)], ALU.subtract)
+                for w, (g, lst) in enumerate(((g1, n1_l), (g2, n2_l))):
+                    if (hf, t, w) in ((0, 3, 1),):
+                        nc.vector.tensor_copy(g[:], h[t][:].indirect(half_list(lst, hf)))
+                    else:
+                        nc.scalar.activation(g[:], h[t][:].indirect(half_list(lst, hf)), ACT.Copy)
+                eng = nc.gpsimd if (hf, t) in ((0, 0), (0, 1)) else nc.vector
+                eng.tensor_tensor(pa[:, cols(t)], h[t][:, cols(hf)], g1[:], ALU.subtract)
+                eng.tensor_tensor(pb[:, cols(t)], g2[:], h[t][:, cols(hf)], ALU.subtract)
             lo = sb("lo%d" % hf, TILES * HALF, BF16)
             hi = sb("hi%d" % hf, TILES * HALF, BF16)
             up = sb("up%d" % hf, TILES * HALF, BF16)
             z = sb("z%d" % hf, TILES * HALF, BF16)
-            zi = sb("zi%d" % hf, TILES * HALF, BF16)
             z_w = sb("z_w%d" % hf, HALF, U32)
             z_b = sb("z_b%d" % hf, HALF, U8)
             pieces = hf + 1
             width = HALF // pieces
+            zi = [sb("zi%d_%d" % (hf, k), TILES * width, BF16) for k in range(pieces)]
 
             def part(tile, k):
                 return tile[:].rearrange("p (t j) -> p t j", t=TILES)[:, :, width * k : width * (k + 1)]
@@ -176,62 +179,65 @@ def tile_picked_pqcjpullbminmod_none_p_kernel(tc, x_words, x_scales, d_words, d_
                 nc.vector.tensor_tensor(part(z, k), part(up, k), part(hi, k), ALU.min)
             for k in range(pieces):
                 nc.vector.tensor_copy(
-                    zi[:, 4 * width * k : 4 * width * (k + 1)].rearrange("p (c i t) -> p c t i", t=4, i=4),
+                    zi[k][:].rearrange("p (c i t) -> p c t i", t=4, i=4),
                     part(z, k).rearrange("p t (c i) -> p c t i", i=4),
                 )
             for k in range(pieces):
                 c = slice(width * k, width * (k + 1))
-                nc.vector.quantize_mx(out=z_w[:, c].bitcast(FP8X4), scales=z_b[:, c], in_=zi[:, 4 * width * k : 4 * width * (k + 1)])
+                nc.vector.quantize_mx(out=z_w[:, c].bitcast(FP8X4), scales=z_b[:, c], in_=zi[k][:])
             z_mx.append((z_w, z_b))
             if hf == 0:
                 a_product(0)
 
-        def block(k):
-            return slice(P * k, P * (k + 1))
-
-        bn = []
-        for t in range(TILES):
-            bn_t = sb("bn%d" % t, N, F32)
-            nc.scalar.activation(bn_t[:], b_banks[t][:], ACT.Copy, scale=-0.0625)
-            bn.append(bn_t)
-        g4_slots = ["", "z1", "zi1", "z_w1"]
-        db_banks = []
+        bs = [sb("b%d" % t, N, F32) for t in range(TILES)]
         a_half = [sb("a%d" % t, N, F32) for t in range(TILES)]
-
-        def gate(t):
-            g4 = sb("g4_%d" % t, N, F32, tag=g4_slots[t])
-            for hf in range(2):
-                window = bn[t][:].indirect(half_list(n4_l, hf))
-                if t in (0, 3):
-                    nc.scalar.activation(g4[:, cols(hf)], window, ACT.Copy, scale=-1.0)
-                else:
-                    nc.vector.tensor_scalar(g4[:, cols(hf)], window, -1.0, 0.0, ALU.mult, ALU.add)
-            bank = psum.tile([P, N], F32, name="bank_db", tag="bank%d" % (TILES + t))
-            for k in range(TILES):
-                nc.tensor.matmul(bank[:, block(k)], lhsT=bn[t][:, block(k)], rhs=ident[:], is_transpose=True, start=True, stop=False)
-                nc.tensor.matmul(bank[:, block(k)], lhsT=g4[:, block(k)], rhs=ident[:], is_transpose=True, start=False, stop=True)
-            db_banks.append(bank)
-
+        g4_slots = ["", "z1", "zi1_0", "z_w1"]
+        db_slots = ["zi1_1", "", "", ""]
+        g4 = {}
+        db = {}
+        th = {}
         out_v = out.rearrange("(c t i) j -> t c i j", t=TILES, i=8)
+
+        def b_out(t):
+            nc.scalar.activation(bs[t][:], b_banks[t][:], ACT.Copy, scale=0.0625)
+
+        def a_first():
+            for t in range(TILES):
+                nc.scalar.activation(a_half[t][:, cols(0)], a_banks[t][:, cols(0)], ACT.Copy, scale=0.03125)
+
+        def fetch(t):
+            g4[t] = sb("g4_%d" % t, N, F32, tag=g4_slots[t])
+            for hf in range(2):
+                window = bs[t][:].indirect(half_list(n4_l, hf))
+                if (t, hf) in ((0, 0), (0, 1)):
+                    nc.scalar.activation(g4[t][:, cols(hf)], window, ACT.Copy)
+                else:
+                    nc.vector.tensor_copy(g4[t][:, cols(hf)], window)
+
+        def diff(t):
+            db[t] = sb("db%d" % t, N, F32, tag=db_slots[t])
+            (nc.gpsimd if t in (0, 1, 2, 3) else nc.vector).tensor_tensor(db[t][:], g4[t][:], bs[t][:], ALU.subtract)
+
+        def squash(t):
+            th[t] = sb("th%d" % t, N, F32)
+            nc.scalar.activation(th[t][:], db[t][:], ACT.Tanh, scale=0.5)
 
         def finish(t):
             a_t = a_half[t]
             nc.scalar.activation(a_t[:, cols(1)], a_banks[t][:, cols(1)], ACT.Copy, scale=0.03125)
-            th_t = sb("th%d" % t, N, F32, tag="z_b1" if t == 0 else "")
-            nc.scalar.activation(th_t[:], db_banks[t][:], ACT.Tanh, scale=0.5)
-            th_bank = psum.tile([P, N], F32, name="bank_th", tag="bank%d" % (TILES + t))
-            for k in range(TILES):
-                nc.tensor.transpose(th_bank[:, block(k)], th_t[:, block(k)], ident[:])
             g3 = sb("g3_%d" % t, N, F32)
             for hf in range(2):
-                nc.scalar.activation(g3[:, cols(hf)], a_t[:].indirect(half_list(n3_l, hf)), ACT.Copy)
-            da = sb("da%d" % t, N, F32)
+                if (t, hf) in ():
+                    nc.vector.tensor_copy(g3[:, cols(hf)], a_t[:].indirect(half_list(n3_l, hf)))
+                else:
+                    nc.scalar.activation(g3[:, cols(hf)], a_t[:].indirect(half_list(n3_l, hf)), ACT.Copy)
+            da = sb("da%d" % t, N, F32, tag="da")
             mv = sb("mv%d" % t, N, F32)
             o = sb("o%d" % t, N, F32)
             for hf in range(2):
-                nc.vector.tensor_tensor(da[:, cols(hf)], g3[:, cols(hf)], a_t[:, cols(hf)], ALU.subtract)
+                nc.vector.scalar_tensor_tensor(da[:, cols(hf)], a_banks[t][:, cols(hf)], -0.03125, g3[:, cols(hf)], ALU.mult, ALU.add)
             for hf in range(2):
-                nc.vector.scalar_tensor_tensor(mv[:, cols(hf)], th_bank[:, cols(hf)], 1.0, da[:, cols(hf)], ALU.add, ALU.mult)
+                nc.vector.scalar_tensor_tensor(mv[:, cols(hf)], th[t][:, cols(hf)], 1.0, da[:, cols(hf)], ALU.add, ALU.mult)
             for hf in range(2):
                 nc.vector.scalar_tensor_tensor(o[:, cols(hf)], a_banks[t][:, cols(hf)], 0.0625, mv[:, cols(hf)], ALU.mult, ALU.add)
                 if t == TILES - 1:
@@ -239,13 +245,25 @@ def tile_picked_pqcjpullbminmod_none_p_kernel(tc, x_words, x_scales, d_words, d_
             if t < TILES - 1:
                 nc.sync.dma_start(out_v[t], o[:])
 
-        gate(0)
-        for t in range(TILES):
-            nc.scalar.activation(a_half[t][:, cols(0)], a_banks[t][:, cols(0)], ACT.Copy, scale=0.03125)
+        b_out(0)
+        fetch(0)
+        b_out(1)
+        a_first()
+        b_out(2)
+        b_out(3)
         a_product(1)
-        gate(1)
-        gate(2)
+        diff(0)
+        fetch(1)
+        diff(1)
+        fetch(2)
+        diff(2)
+        fetch(3)
+        diff(3)
+        squash(0)
         finish(0)
-        gate(3)
-        for t in range(1, TILES):
-            finish(t)
+        squash(1)
+        finish(1)
+        squash(2)
+        finish(2)
+        squash(3)
+        finish(3)

@@ -216,7 +216,10 @@ def tile_picked_pqcjpullbminmod_none_p_kernel(tc, x_words, x_scales, d_words, d_
 
         def diff(t):
             db[t] = sb("db%d" % t, N, F32, tag=db_slots[t])
-            (nc.gpsimd if t in (0, 1, 2, 3) else nc.vector).tensor_tensor(db[t][:], g4[t][:], bs[t][:], ALU.subtract)
+            if t in (0, 1, 2):
+                nc.gpsimd.tensor_tensor(db[t][:], g4[t][:], bs[t][:], ALU.subtract)
+            else:
+                nc.vector.scalar_tensor_tensor(db[t][:], b_banks[t][:], -0.0625, g4[t][:], ALU.mult, ALU.add)
 
         def squash(t):
             th[t] = sb("th%d" % t, N, F32)
@@ -227,7 +230,7 @@ def tile_picked_pqcjpullbminmod_none_p_kernel(tc, x_words, x_scales, d_words, d_
             nc.scalar.activation(a_t[:, cols(1)], a_banks[t][:, cols(1)], ACT.Copy, scale=0.03125)
             g3 = sb("g3_%d" % t, N, F32)
             for hf in range(2):
-                if (t, hf) in ():
+                if (t, hf) in ((0, 1),):
                     nc.vector.tensor_copy(g3[:, cols(hf)], a_t[:].indirect(half_list(n3_l, hf)))
                 else:
                     nc.scalar.activation(g3[:, cols(hf)], a_t[:].indirect(half_list(n3_l, hf)), ACT.Copy)

from contextlib import ExitStack

import concourse.mybir as mybir

F32 = mybir.dt.float32
BF16 = mybir.dt.bfloat16
I32 = mybir.dt.int32
U32 = mybir.dt.uint32
U16 = mybir.dt.uint16
U8 = mybir.dt.uint8
FP8X4 = mybir.dt.float8_e4m3fn_x4
ALU = mybir.AluOpType
ACT = mybir.ActivationFunctionType

P = 128
N = 512
TILES = 4
HALF = 256
TOKENS = 1024
CODES = 2048
FLOPS = 3 * 2 * 512 * 512 * 512


def tile_picked_pqcjpullbminmod_none_p_kernel(tc, x_words, x_scales, d_words, d_scales, gs, offs, k1, n1, n2, cand, two, k2, n3, n4, out):
    nc = tc.nc
    with ExitStack() as ctx:
        lists = ctx.enter_context(tc.tile_pool(name="lists", bufs=1))
        keep = ctx.enter_context(tc.tile_pool(name="keep", bufs=1))
        psum = ctx.enter_context(tc.psum_pool(name="psum", bufs=1))

        def load_list(name, src):
            t = lists.tile([P, N // 16], U16, name=name)
            nc.sync.dma_start(t[:], src)
            return t

        def sb(name, width, dtype, tag=""):
            return keep.tile([P, width], dtype, name=name, tag=tag or name, align_bytes=64)

        def half_list(t, hf):
            return t[:, 16 * hf : 16 * (hf + 1)]

        def cols(hf):
            return slice(HALF * hf, HALF * (hf + 1))

        k1_l = load_list("k1_l", k1)
        d_sc = sb("d_sc", CODES, U8)
        nc.sync.dma_start(
            d_sc[:].bitcast(I32),
            d_scales.rearrange("z q c -> q z c").bitcast(I32).to_broadcast([16, 8, CODES // 4]),
        )
        offs_l = load_list("offs_l", offs)
        x_w = sb("x_w", TOKENS, U32)
        nc.sync.dma_start(x_w[:].bitcast(I32), x_words[0].rearrange("p n t -> p (n t)").bitcast(I32))
        d_w = sb("d_w", CODES, U32)
        nc.sync.dma_start(d_w[:].bitcast(I32), d_words[0].rearrange("p n t -> p (n t)").bitcast(I32))
        x_sc = sb("x_sc", TOKENS, U8)
        for q in range(4):
            nc.sync.dma_start(
                x_sc[32 * q : 32 * (q + 1), :].bitcast(I32),
                x_scales[:, 4 * q : 4 * q + 4, :].bitcast(I32).to_broadcast([8, 4, TOKENS // 4]),
            )
        k2_l = load_list("k2_l", k2)
        two_l = load_list("two_l", two)
        cand_l = load_list("cand_l", cand)
        gs_sb = sb("gs_sb", TILES, F32)
        nc.gpsimd.dma_start(gs_sb[:], gs.rearrange("(p t) o -> p (t o)", t=TILES))
        n1_l = load_list("n1_l", n1)
        n2_l = load_list("n2_l", n2)
        n4_l = load_list("n4_l", n4)
        n3_l = load_list("n3_l", n3)

        gsc = sb("gsc", TILES, F32)
        nc.gpsimd.tensor_scalar(gsc[:], gs_sb[:], 0.0625, 0.0, ALU.mult, ALU.add)

        def gather(name, window, lst, dtype):
            t = sb(name, N, dtype)
            nc.vector.tensor_copy(t[:], window[:].indirect(lst[:]))
            return t

        def place_odd_rows(plane, queue):
            for j in range(1, 4):
                queue.dma_start(plane[j:P:32, :].bitcast(I32), plane[8 * j : P : 32, :].bitcast(I32))

        def mx(bank, w, s, t, rw, rs):
            m = slice(P * t, P * (t + 1))
            nc.tensor.matmul_mx(out=bank, lhsT=w[:, m].bitcast(FP8X4), lhsT_scale=s[:, m], rhs=rw.bitcast(FP8X4), rhs_scale=rs, start=True, stop=True)

        k1_bg = gather("k1_bg", d_sc, k1_l, U8)
        k1_b = sb("k1_b", N, U8)
        nc.vector.tensor_copy(
            k1_b[:].rearrange("p (t c i) -> p c t i", t=4, i=16), k1_bg[:].rearrange("p (c i t) -> p c t i", t=4, i=16)
        )
        place_odd_rows(k1_b, nc.scalar)
        offs_w = gather("offs_w", x_w, offs_l, U32)
        k1_wg = gather("k1_wg", d_w, k1_l, U32)
        k1_w = sb("k1_w", N, U32)
        nc.vector.tensor_copy(
            k1_w[:].bitcast(I32).rearrange("p (t c i) -> p c t i", t=4, i=4),
            k1_wg[:].bitcast(I32).rearrange("p (c i t) -> p c t i", t=4, i=4),
        )
        offs_b = gather("offs_b", x_sc, offs_l, U8)
        h = []
        for t in range(TILES):
            bank = psum.tile([P, N], F32, name="bank_h", tag="bank%d" % t)
            mx(bank[:], k1_w, k1_b, t, offs_w[:], offs_b[:])
            h_t = sb("h%d" % t, N, F32)
            nc.scalar.activation(h_t[:], bank[:], ACT.Copy, scale=gsc[:, t : t + 1])
            h.append(h_t)

        k2_wg = gather("k2_wg", d_w, k2_l, U32)
        k2_bg = gather("k2_bg", d_sc, k2_l, U8)
        cand_bg = gather("cand_bg", x_sc, cand_l, U8)
        k2_w = sb("k2_w", N, U32)
        nc.vector.tensor_copy(
            k2_w[:].bitcast(I32).rearrange("p (t c i) -> p c t i", t=4, i=8),
            k2_wg[:].bitcast(I32).rearrange("p (c t i) -> p c t i", t=4, i=8),
        )
        k2_b = sb("k2_b", N, U8)
        nc.vector.tensor_copy(
            k2_b[:].bitcast(I32).rearrange("p (t c i) -> p c t i", t=4, i=2),
            k2_bg[:].bitcast(I32).rearrange("p (c t i) -> p c t i", t=4, i=2),
        )
        place_odd_rows(k2_b, nc.sync)
        cand_b = sb("cand_b", N, U8)
        nc.vector.tensor_copy(
            cand_b[:].bitcast(I32).rearrange("p (t c i) -> p c t i", t=4, i=2),
            cand_bg[:].bitcast(I32).rearrange("p (c t i) -> p c t i", t=4, i=2),
        )
        two_b = gather("two_b", x_sc, two_l, U8)
        two_w = gather("two_w", x_w, two_l, U32)
        b_banks = []
        for t in range(TILES):
            bank = psum.tile([P, N], F32, name="bank_b", tag="bank%d" % (TILES + t))
            mx(bank[:], k2_w, k2_b, t, two_w[:], two_b[:])
            b_banks.append(bank)
        cand_w = sb("cand_w", N, U32)
        nc.vector.tensor_copy(cand_w[:].rearrange("p (t c i) -> p c t i", t=4, i=8), x_w[:].indirect(cand_l[:]))

        a_banks = [psum.tile([P, N], F32, name="bank_a", tag="bank%d" % t) for t in range(TILES)]
        z_mx = []

        def a_product(hf):
            for t in range(TILES):
                mx(a_banks[t][:, cols(hf)], cand_w, cand_b, t, z_mx[hf][0][:], z_mx[hf][1][:])

        for hf in range(2):
            pa = sb("pa%d" % hf, TILES * HALF, BF16)
            pb = sb("pb%d" % hf, TILES * HALF, BF16)
            for t in range(TILES):
                g1 = sb("g1_%d_%d" % (hf, t), HALF, F32)
                g2 = sb("g2_%d_%d" % (hf, t), HALF, F32)
                for w, (g, lst) in enumerate(((g1, n1_l), (g2, n2_l))):
                    if (hf, t, w) in ((0, 3, 1),):
                        nc.vector.tensor_copy(g[:], h[t][:].indirect(half_list(lst, hf)))
                    else:
                        nc.scalar.activation(g[:], h[t][:].indirect(half_list(lst, hf)), ACT.Copy)
                eng = nc.gpsimd if (hf, t) in ((0, 0), (0, 1)) else nc.vector
                eng.tensor_tensor(pa[:, cols(t)], h[t][:, cols(hf)], g1[:], ALU.subtract)
                eng.tensor_tensor(pb[:, cols(t)], g2[:], h[t][:, cols(hf)], ALU.subtract)
            lo = sb("lo%d" % hf, TILES * HALF, BF16)
            hi = sb("hi%d" % hf, TILES * HALF, BF16)
            up = sb("up%d" % hf, TILES * HALF, BF16)
            z = sb("z%d" % hf, TILES * HALF, BF16)
            z_w = sb("z_w%d" % hf, HALF, U32)
            z_b = sb("z_b%d" % hf, HALF, U8)
            pieces = hf + 1
            width = HALF // pieces
            zi = [sb("zi%d_%d" % (hf, k), TILES * width, BF16) for k in range(pieces)]

            def part(tile, k):
                return tile[:].rearrange("p (t j) -> p t j", t=TILES)[:, :, width * k : width * (k + 1)]

            for k in range(pieces):
                nc.vector.tensor_scalar_min(part(lo, k), part(pa, k), 0.0)
                nc.vector.tensor_scalar_max(part(hi, k), part(pa, k), 0.0)
            for k in range(pieces):
                nc.vector.tensor_tensor(part(up, k), part(pb, k), part(lo, k), ALU.max)
            for k in range(pieces):
                nc.vector.tensor_tensor(part(z, k), part(up, k), part(hi, k), ALU.min)
            for k in range(pieces):
                nc.vector.tensor_copy(
                    zi[k][:].rearrange("p (c i t) -> p c t i", t=4, i=4),
                    part(z, k).rearrange("p t (c i) -> p c t i", i=4),
                )
            for k in range(pieces):
                c = slice(width * k, width * (k + 1))
                nc.vector.quantize_mx(out=z_w[:, c].bitcast(FP8X4), scales=z_b[:, c], in_=zi[k][:])
            z_mx.append((z_w, z_b))
            if hf == 0:
                a_product(0)

        bs = [sb("b%d" % t, N, F32) for t in range(TILES)]
        a_half = [sb("a%d" % t, N, F32) for t in range(TILES)]
        g4_slots = ["", "z1", "zi1_0", "z_w1"]
        db_slots = ["zi1_1", "", "", ""]
        g4 = {}
        db = {}
        th = {}
        out_v = out.rearrange("(c t i) j -> t c i j", t=TILES, i=8)

        def b_out(t):
            nc.scalar.activation(bs[t][:], b_banks[t][:], ACT.Copy, scale=0.0625)

        def a_first():
            for t in range(TILES):
                nc.scalar.activation(a_half[t][:, cols(0)], a_banks[t][:, cols(0)], ACT.Copy, scale=0.03125)

        def fetch(t):
            g4[t] = sb("g4_%d" % t, N, F32, tag=g4_slots[t])
            for hf in range(2):
                window = bs[t][:].indirect(half_list(n4_l, hf))
                if (t, hf) in ((0, 0), (0, 1)):
                    nc.scalar.activation(g4[t][:, cols(hf)], window, ACT.Copy)
                else:
                    nc.vector.tensor_copy(g4[t][:, cols(hf)], window)

        def diff(t):
            db[t] = sb("db%d" % t, N, F32, tag=db_slots[t])
            if t in (0, 1, 2):
                nc.gpsimd.tensor_tensor(db[t][:], g4[t][:], bs[t][:], ALU.subtract)
            else:
                nc.vector.scalar_tensor_tensor(db[t][:], b_banks[t][:], -0.0625, g4[t][:], ALU.mult, ALU.add)

        def squash(t):
            th[t] = sb("th%d" % t, N, F32)
            nc.scalar.activation(th[t][:], db[t][:], ACT.Tanh, scale=0.5)

        def finish(t):
            a_t = a_half[t]
            nc.scalar.activation(a_t[:, cols(1)], a_banks[t][:, cols(1)], ACT.Copy, scale=0.03125)
            g3 = sb("g3_%d" % t, N, F32)
            for hf in range(2):
                if (t, hf) in ((0, 1),):
                    nc.vector.tensor_copy(g3[:, cols(hf)], a_t[:].indirect(half_list(n3_l, hf)))
                else:
                    nc.scalar.activation(g3[:, cols(hf)], a_t[:].indirect(half_list(n3_l, hf)), ACT.Copy)
            da = sb("da%d" % t, N, F32, tag="da")
            mv = sb("mv%d" % t, N, F32)
            o = sb("o%d" % t, N, F32)
            for hf in range(2):
                nc.vector.scalar_tensor_tensor(da[:, cols(hf)], a_banks[t][:, cols(hf)], -0.03125, g3[:, cols(hf)], ALU.mult, ALU.add)
            for hf in range(2):
                nc.vector.scalar_tensor_tensor(mv[:, cols(hf)], th[t][:, cols(hf)], 1.0, da[:, cols(hf)], ALU.add, ALU.mult)
            for hf in range(2):
                nc.vector.scalar_tensor_tensor(o[:, cols(hf)], a_banks[t][:, cols(hf)], 0.0625, mv[:, cols(hf)], ALU.mult, ALU.add)
                if t == TILES - 1:
                    nc.sync.dma_start(out_v[t][:, :, cols(hf)], o[:, cols(hf)])
            if t < TILES - 1:
                nc.sync.dma_start(out_v[t], o[:])

        b_out(0)
        fetch(0)
        b_out(1)
        a_first()
        b_out(2)
        b_out(3)
        a_product(1)
        diff(0)
        fetch(1)
        diff(1)
        fetch(2)
        diff(2)
        fetch(3)
        diff(3)
        squash(0)
        finish(0)
        squash(1)
        finish(1)
        squash(2)
        finish(2)
        squash(3)
        finish(3)
